import numpy as np
import ml_dtypes


def mxq(x, axis, fmt="e4m3"):
    dtype, down = {"e4m3": (ml_dtypes.float8_e4m3fn, 7), "e5m2": (ml_dtypes.float8_e5m2, 14)}[fmt]
    v = np.moveaxis(np.asarray(x, np.float32).astype(ml_dtypes.bfloat16).astype(np.float64), axis, -1)
    blocks = v.reshape(v.shape[:-1] + (-1, 32))
    amax = np.abs(blocks).max(-1, keepdims=True)
    byte = np.maximum(np.where(amax > 0, np.frexp(amax)[1] - 1 + 127, 0) - down, 1)
    scale = np.exp2(byte - 127.0)
    codes = (blocks / scale).astype(np.float32).astype(dtype).astype(np.float64)
    return np.moveaxis((codes * scale).reshape(v.shape), -1, axis)


WIDE = False


def mx_kscale(k):
    if not WIDE:
        return np.ones(k)
    levels = np.array([10, -10, 5, -5, 0])
    if k % 512:
        return np.exp2(np.random.permutation(np.resize(levels, k // 32))).repeat(32)
    a = np.empty((k // 512, 16))
    for p in range(k // 512):
        a[p, :8] = np.random.permutation(np.resize(levels, 8))
        for g in range(8):
            far = levels[np.abs(levels - a[p, g]) >= 10]
            a[p, g + 8] = far[np.random.randint(len(far))]
    return np.exp2(a.ravel()).repeat(32)


def f64(x):
    return np.asarray(x).astype(np.float64)


def striped(idx):
    return np.tile(np.asarray(idx).reshape(-1, 16).T, (8, 1)).astype(np.uint16)


def unstriped(offs):
    return offs[:16].T.reshape(-1).astype(np.int64)


E2M1 = np.array([0.0, 0.5, 1.0, 1.5, 2.0, 3.0, 4.0, 6.0, -0.0, -0.5, -1.0, -1.5, -2.0, -3.0, -4.0, -6.0])


def pack_weight(w, fmt):
    k, n = w.shape
    w = f64(np.asarray(w, np.float32).astype(ml_dtypes.bfloat16)).reshape(k // 32, 32, n)
    amax = np.abs(w).max(1)
    if fmt == "e4m3":
        byte = np.frexp(amax)[1] - 1 + 127 - 7
    else:
        mant, ex = np.frexp(amax / 6.0)
        byte = np.where(mant > 0.5, ex, ex - 1) + 127
    byte = np.clip(np.where(amax > 0, byte, 1), 1, 254)
    scaled = (w * np.exp2(127.0 - byte)[:, None, :]).reshape(k, n).astype(np.float32)
    by_word = np.ascontiguousarray(scaled.reshape(k // 512, 128, 4, n).transpose(0, 1, 3, 2))
    if fmt == "e4m3":
        words = by_word.astype(ml_dtypes.float8_e4m3fn).view(np.uint8)
    else:
        c = by_word.astype(ml_dtypes.float4_e2m1fn).view(np.uint8) & 0xF
        words = (c[..., 0::2] | (c[..., 1::2] << 4)).reshape(k // 512, 128, 2 * n)
    return np.ascontiguousarray(words), np.ascontiguousarray(byte.astype(np.uint8).reshape(k // 512, 16, n))


def unpack_weight(words, scales, fmt):
    g, _, n = scales.shape
    words = np.ascontiguousarray(words).reshape(g, 128, n, -1)
    if fmt == "e4m3":
        vals = words.view(ml_dtypes.float8_e4m3fn).astype(np.float64)
    else:
        nib = np.empty((g, 128, n, 4), np.uint8)
        nib[..., 0::2] = words & 0xF
        nib[..., 1::2] = words >> 4
        vals = E2M1[nib]
    vals = vals * np.repeat(np.exp2(scales.astype(np.float64) - 127.0), 8, axis=1)[..., None]
    return vals.transpose(0, 1, 3, 2).reshape(g * 512, n)


B, N, T, D, NQ = 1, 512, 2048, 1024, 128


def setup_inputs():
    n = np.random.standard_normal
    idx = np.random.permutation(T)[:B * N]
    s = mx_kscale(D)[:, None]
    kp = pack_weight(n((D, T)) / s, "e2m1")
    return {
        "qT": (n((B, D, NQ)) * s * (0.70 / np.sqrt(D))).astype(np.float32),
        "k_words": np.ascontiguousarray(kp[0].reshape(1, 2, 128, T, 2).transpose(0, 2, 3, 1, 4)).reshape(1, 128, T, 4),
        "k_scales": kp[1],
        "offs": striped(idx),
    }


def reference(qT, k_words, k_scales, offs):
    idx = unstriped(offs)
    pick = lambda x, which: x[:, which].reshape(x.shape[0], B, -1).transpose(1, 0, 2)
    k = unpack_weight(k_words.reshape(1, 128, T, 2, 2).transpose(0, 3, 1, 2, 4).reshape(2, 128, 2 * T), k_scales, "e2m1")
    kg = pick(k, idx)
    qq = mxq(f64(qT), 1, "e4m3")
    a = qq.transpose(0, 2, 1) @ kg
    x = 1.0 + a + 0.5 * np.square(a)
    y = x / np.sum(x, axis=-1, keepdims=True)
    return y

@@ -1,0 +1,126 @@
+from contextlib import ExitStack
+
+import concourse.mybir as mybir
+
+F32 = mybir.dt.float32
+BF16 = mybir.dt.bfloat16
+I32 = mybir.dt.int32
+U32 = mybir.dt.uint32
+U16 = mybir.dt.uint16
+U8 = mybir.dt.uint8
+FP8X4 = mybir.dt.float8_e4m3fn_x4
+FP4X4 = mybir.dt.float4_e2m1fn_x4
+ADD = mybir.AluOpType.add
+MULT = mybir.AluOpType.mult
+SQUARE = mybir.ActivationFunctionType.Square
+
+P = 128
+PACK = 4
+K_PASS = P * PACK
+D, T, N, NQ = 1024, 2048, 512, 128
+PASSES = D // K_PASS
+HALF = N // 2
+GROUP = 128
+
+FLOPS = 2 * NQ * N * D
+
+
+def tile_attend_nrm_taylor_topk_kernel(tc, qT, k_words, k_scales, offs, out):
+    nc = tc.nc
+    with ExitStack() as ctx:
+        keep = ctx.enter_context(tc.tile_pool(name="keep", bufs=1))
+        psum = ctx.enter_context(tc.psum_pool(name="psum", bufs=1))
+
+        offsets = keep.tile([P, N // 16], U16, name="offsets")
+        nc.sync.dma_start(offsets[:], offs)
+
+        scale_pool = keep.tile([P, T // 4], I32, name="scale_pool", align_bytes=64)
+        nc.vector.memset(scale_pool[:], 0)
+        scale_rows = k_scales.bitcast(I32).rearrange("o (b r) t -> r b o t", r=4)
+        for r in range(4):
+            nc.scalar.dma_start(scale_pool[r:P:16, :], scale_rows[r])
+
+        word_pool = keep.tile([P, T], I32, name="word_pool", align_bytes=64)
+        nc.sync.dma_start(word_pool[:], k_words[0].rearrange("p t b -> p (t b)").bitcast(I32))
+
+        q_raw = []
+        for o in range(PASSES):
+            raw = keep.tile([P, PACK, NQ], F32, name=f"q_raw{o}", align_bytes=64)
+            nc.sync.dma_start(raw[:], qT[0, o * K_PASS : (o + 1) * K_PASS, :].rearrange("(p j) w -> p j w", j=PACK))
+            q_raw.append(raw)
+
+        second_plane = keep.tile([P, N // 4], I32, name="second_plane", align_bytes=64)
+        nc.vector.memset(second_plane[:], 0)
+        seed = keep.tile([P, 1], F32, name="seed")
+        nc.vector.memset(seed[:], 1.0)
+        one = keep.tile([P, 1], F32, name="one")
+        nc.scalar.activation(one[:], seed[:], SQUARE)
+
+        picked_scales = keep.tile([P, N], U8, name="picked_scales", align_bytes=64)
+        nc.vector.tensor_copy(picked_scales[:], scale_pool[:].bitcast(U8).indirect(offsets[:]))
+        for r in range(4):
+            nc.sync.dma_start(second_plane[r:P:32, :], picked_scales[:].bitcast(I32)[16 + r : P : 32, :])
+        planes = [picked_scales[:], second_plane[:].bitcast(U8)]
+
+        picked_words = []
+        for h in range(2):
+            picked = keep.tile([P, HALF], U32, name=f"picked_words{h}", align_bytes=64)
+            cols = slice(h * HALF // 16, (h + 1) * HALF // 16)
+            nc.vector.tensor_copy(picked[:], word_pool[:].bitcast(U32).indirect(offsets[:, cols]))
+            picked_words.append(picked)
+
+        keys = []
+        for h in range(2):
+            parted = keep.tile([P, PASSES, 2 * HALF], U8, name=f"keys{h}", align_bytes=64)
+            nc.vector.tensor_copy(
+                parted[:].bitcast(U16),
+                picked_words[h][:].bitcast(U16).rearrange("p (n o) -> p o n", o=PASSES),
+            )
+            keys.append(parted)
+
+        q_codes, q_scales = [], []
+        for o in range(PASSES):
+            grouped = keep.tile([P, NQ, PACK], BF16, name=f"q_grouped{o}", align_bytes=64)
+            nc.scalar.copy(
+                grouped[:].rearrange("p (c i) t -> p c t i", i=4),
+                q_raw[o][:].rearrange("p t (c i) -> p c t i", i=4),
+            )
+            codes = keep.tile([P, NQ], U32, name=f"q_codes{o}", align_bytes=64)
+            scales = keep.tile([P, NQ], U8, name=f"q_scales{o}", align_bytes=64)
+            nc.vector.quantize_mx(
+                out=codes[:].bitcast(FP8X4), scales=scales[:], in_=grouped[:].rearrange("p w j -> p (w j)")
+            )
+            q_codes.append(codes)
+            q_scales.append(scales)
+
+        squares = keep.tile([P, N], F32, name="squares", align_bytes=64)
+        groups = N // GROUP
+        sums = keep.tile([P, groups + 1], F32, name="sums")
+        nc.vector.memset(sums[:, groups : groups + 1], float(N))
+        banks = [psum.tile([P, GROUP], F32, name=f"scores{g}") for g in range(groups)]
+        for o in range(PASSES):
+            for g in range(groups):
+                h, first = divmod(g * GROUP, HALF)
+                nc.tensor.matmul_mx(
+                    out=banks[g][:],
+                    lhsT=q_codes[o][:].bitcast(FP8X4),
+                    lhsT_scale=q_scales[o][:],
+                    rhs=keys[h][:, o, 2 * first : 2 * (first + GROUP)].bitcast(FP4X4),
+                    rhs_scale=planes[o][:, g * GROUP : (g + 1) * GROUP],
+                    start=(o == 0),
+                    stop=(o == PASSES - 1),
+                )
+        for g in range(groups):
+            nc.scalar.activation(
+                squares[:, g * GROUP : (g + 1) * GROUP], banks[g][:], SQUARE, bias=one[:], accum_out=sums[:, g : g + 1]
+            )
+
+        denom = keep.tile([P, 1], F32, name="denom")
+        nc.vector.tensor_reduce(denom[:], sums[:], mybir.AxisListType.X, ADD)
+        inverse = keep.tile([P, 1], F32, name="inverse")
+        nc.vector.reciprocal(inverse[:], denom[:])
+        for h, queue in enumerate((nc.sync, nc.scalar)):
+            cols = slice(h * HALF, (h + 1) * HALF)
+            weights = keep.tile([P, HALF], F32, name=f"weights{h}", align_bytes=64)
+            nc.vector.tensor_scalar(weights[:], squares[:, cols], 1.0, inverse[:], ADD, MULT)
+            queue.dma_start(out[0, :, cols], weights[:])

@@ -21,6 +21,7 @@ D, T, N, NQ = 1024, 2048, 512, 128
 PASSES = D // K_PASS
 HALF = N // 2
 GROUP = 128
+GROUPS = N // GROUP
 
 FLOPS = 2 * NQ * N * D
 
@@ -29,32 +30,38 @@ def tile_attend_nrm_taylor_topk_kernel(tc, qT, k_words, k_scales, offs, out):
     nc = tc.nc
     with ExitStack() as ctx:
         keep = ctx.enter_context(tc.tile_pool(name="keep", bufs=1))
+        late = ctx.enter_context(tc.tile_pool(name="late", bufs=1))
         psum = ctx.enter_context(tc.psum_pool(name="psum", bufs=1))
 
         offsets = keep.tile([P, N // 16], U16, name="offsets")
         nc.sync.dma_start(offsets[:], offs)
 
+        def load_queries(o, raw):
+            rows = qT[0, o * K_PASS : (o + 1) * K_PASS, :]
+            nc.sync.dma_start(raw[:], rows.rearrange("(p j) w -> p j w", j=PACK))
+
+        q_first = keep.tile([P, PACK, NQ], F32, name="q_first", align_bytes=64)
+        load_queries(0, q_first)
+
+        shares = late.tile([P, 16], F32, name="shares", offset=4 * T - 32)
+        nc.vector.memset(shares[:], N / 16)
         scale_pool = keep.tile([P, T // 4], I32, name="scale_pool", align_bytes=64)
         nc.vector.memset(scale_pool[:], 0)
         scale_rows = k_scales.bitcast(I32).rearrange("o (b r) t -> r b o t", r=4)
         for r in range(4):
-            nc.scalar.dma_start(scale_pool[r:P:16, :], scale_rows[r])
+            nc.sync.dma_start(scale_pool[r:P:16, :], scale_rows[r])
+        sums = keep.tile([P, GROUPS + 1], F32, name="sums")
+        nc.vector.tensor_reduce(sums[:, GROUPS : GROUPS + 1], shares[:], mybir.AxisListType.X, ADD)
 
-        word_pool = keep.tile([P, T], I32, name="word_pool", align_bytes=64)
+        word_pool = late.tile([P, T], I32, name="word_pool", offset=0, align_bytes=64)
         nc.sync.dma_start(word_pool[:], k_words[0].rearrange("p t b -> p (t b)").bitcast(I32))
-
-        q_raw = []
-        for o in range(PASSES):
-            raw = keep.tile([P, PACK, NQ], F32, name=f"q_raw{o}", align_bytes=64)
-            nc.sync.dma_start(raw[:], qT[0, o * K_PASS : (o + 1) * K_PASS, :].rearrange("(p j) w -> p j w", j=PACK))
-            q_raw.append(raw)
+        q_second = late.tile([P, PACK, NQ], F32, name="q_second", offset=4 * T, align_bytes=64)
+        load_queries(1, q_second)
 
         second_plane = keep.tile([P, N // 4], I32, name="second_plane", align_bytes=64)
         nc.vector.memset(second_plane[:], 0)
-        seed = keep.tile([P, 1], F32, name="seed")
-        nc.vector.memset(seed[:], 1.0)
         one = keep.tile([P, 1], F32, name="one")
-        nc.scalar.activation(one[:], seed[:], SQUARE)
+        nc.scalar.activation(one[:], sums[:, GROUPS : GROUPS + 1], SQUARE, scale=1.0 / N)
 
         picked_scales = keep.tile([P, N], U8, name="picked_scales", align_bytes=64)
         nc.vector.tensor_copy(picked_scales[:], scale_pool[:].bitcast(U8).indirect(offsets[:]))
@@ -62,55 +69,45 @@ def tile_attend_nrm_taylor_topk_kernel(tc, qT, k_words, k_scales, offs, out):
             nc.sync.dma_start(second_plane[r:P:32, :], picked_scales[:].bitcast(I32)[16 + r : P : 32, :])
         planes = [picked_scales[:], second_plane[:].bitcast(U8)]
 
-        picked_words = []
-        for h in range(2):
-            picked = keep.tile([P, HALF], U32, name=f"picked_words{h}", align_bytes=64)
-            cols = slice(h * HALF // 16, (h + 1) * HALF // 16)
-            nc.vector.tensor_copy(picked[:], word_pool[:].bitcast(U32).indirect(offsets[:, cols]))
-            picked_words.append(picked)
-
-        keys = []
-        for h in range(2):
-            parted = keep.tile([P, PASSES, 2 * HALF], U8, name=f"keys{h}", align_bytes=64)
-            nc.vector.tensor_copy(
-                parted[:].bitcast(U16),
-                picked_words[h][:].bitcast(U16).rearrange("p (n o) -> p o n", o=PASSES),
-            )
-            keys.append(parted)
-
-        q_codes, q_scales = [], []
-        for o in range(PASSES):
+        def quantize_queries(o, raw):
             grouped = keep.tile([P, NQ, PACK], BF16, name=f"q_grouped{o}", align_bytes=64)
             nc.scalar.copy(
                 grouped[:].rearrange("p (c i) t -> p c t i", i=4),
-                q_raw[o][:].rearrange("p t (c i) -> p c t i", i=4),
+                raw[:].rearrange("p t (c i) -> p c t i", i=4),
             )
             codes = keep.tile([P, NQ], U32, name=f"q_codes{o}", align_bytes=64)
             scales = keep.tile([P, NQ], U8, name=f"q_scales{o}", align_bytes=64)
             nc.vector.quantize_mx(
                 out=codes[:].bitcast(FP8X4), scales=scales[:], in_=grouped[:].rearrange("p w j -> p (w j)")
             )
-            q_codes.append(codes)
-            q_scales.append(scales)
+            return codes, scales
+
+        queries = [quantize_queries(0, q_first)]
+
+        picked_words = keep.tile([P, N], U32, name="picked_words", align_bytes=64)
+        nc.vector.tensor_copy(picked_words[:], word_pool[:].bitcast(U32).indirect(offsets[:]))
+        word_halves = picked_words[:].bitcast(U16).rearrange("p (n o) -> p o n", o=PASSES)
+        keys = []
+        for o in range(PASSES):
+            parted = keep.tile([P, 2 * N], U8, name=f"keys{o}", align_bytes=64)
+            nc.vector.tensor_copy(parted[:].bitcast(U16), word_halves[:, o, :])
+            keys.append(parted)
+        queries.append(quantize_queries(1, q_second))
 
         squares = keep.tile([P, N], F32, name="squares", align_bytes=64)
-        groups = N // GROUP
-        sums = keep.tile([P, groups + 1], F32, name="sums")
-        nc.vector.memset(sums[:, groups : groups + 1], float(N))
-        banks = [psum.tile([P, GROUP], F32, name=f"scores{g}") for g in range(groups)]
+        banks = [psum.tile([P, GROUP], F32, name=f"scores{g}") for g in range(GROUPS)]
         for o in range(PASSES):
-            for g in range(groups):
-                h, first = divmod(g * GROUP, HALF)
+            for g in range(GROUPS):
                 nc.tensor.matmul_mx(
                     out=banks[g][:],
-                    lhsT=q_codes[o][:].bitcast(FP8X4),
-                    lhsT_scale=q_scales[o][:],
-                    rhs=keys[h][:, o, 2 * first : 2 * (first + GROUP)].bitcast(FP4X4),
+                    lhsT=queries[o][0][:].bitcast(FP8X4),
+                    lhsT_scale=queries[o][1][:],
+                    rhs=keys[o][:, 2 * g * GROUP : 2 * (g + 1) * GROUP].bitcast(FP4X4),
                     rhs_scale=planes[o][:, g * GROUP : (g + 1) * GROUP],
                     start=(o == 0),
                     stop=(o == PASSES - 1),
                 )
-        for g in range(groups):
+        for g in range(GROUPS):
             nc.scalar.activation(
                 squares[:, g * GROUP : (g + 1) * GROUP], banks[g][:], SQUARE, bias=one[:], accum_out=sums[:, g : g + 1]
             )

@@ -13,6 +13,7 @@ FP4X4 = mybir.dt.float4_e2m1fn_x4
 ADD = mybir.AluOpType.add
 MULT = mybir.AluOpType.mult
 SQUARE = mybir.ActivationFunctionType.Square
+INV_SQRT = mybir.ActivationFunctionType.Abs_reciprocal_sqrt
 
 P = 128
 PACK = 4
@@ -33,9 +34,6 @@ def tile_attend_nrm_taylor_topk_kernel(tc, qT, k_words, k_scales, offs, out):
         late = ctx.enter_context(tc.tile_pool(name="late", bufs=1))
         psum = ctx.enter_context(tc.psum_pool(name="psum", bufs=1))
 
-        offsets = keep.tile([P, N // 16], U16, name="offsets")
-        nc.sync.dma_start(offsets[:], offs)
-
         def load_queries(o, raw):
             rows = qT[0, o * K_PASS : (o + 1) * K_PASS, :]
             nc.sync.dma_start(raw[:], rows.rearrange("(p j) w -> p j w", j=PACK))
@@ -43,15 +41,18 @@ def tile_attend_nrm_taylor_topk_kernel(tc, qT, k_words, k_scales, offs, out):
         q_first = keep.tile([P, PACK, NQ], F32, name="q_first", align_bytes=64)
         load_queries(0, q_first)
 
-        shares = late.tile([P, 16], F32, name="shares", offset=4 * T - 32)
-        nc.vector.memset(shares[:], N / 16)
+        offsets = keep.tile([P, N // 16], U16, name="offsets")
+        nc.sync.dma_start(offsets[:], offs)
+
         scale_pool = keep.tile([P, T // 4], I32, name="scale_pool", align_bytes=64)
         nc.vector.memset(scale_pool[:], 0)
         scale_rows = k_scales.bitcast(I32).rearrange("o (b r) t -> r b o t", r=4)
         for r in range(4):
             nc.sync.dma_start(scale_pool[r:P:16, :], scale_rows[r])
-        sums = keep.tile([P, GROUPS + 1], F32, name="sums")
-        nc.vector.tensor_reduce(sums[:, GROUPS : GROUPS + 1], shares[:], mybir.AxisListType.X, ADD)
+        shares = late.tile([P, 16], F32, name="shares", offset=4 * T - 32)
+        nc.vector.memset(shares[:], N / 16)
+        sums = keep.tile([P, GROUPS], F32, name="sums")
+        nc.vector.tensor_reduce(sums[:, GROUPS - 1 : GROUPS], shares[:], mybir.AxisListType.X, ADD)
 
         word_pool = late.tile([P, T], I32, name="word_pool", offset=0, align_bytes=64)
         nc.sync.dma_start(word_pool[:], k_words[0].rearrange("p t b -> p (t b)").bitcast(I32))
@@ -61,7 +62,7 @@ def tile_attend_nrm_taylor_topk_kernel(tc, qT, k_words, k_scales, offs, out):
         second_plane = keep.tile([P, N // 4], I32, name="second_plane", align_bytes=64)
         nc.vector.memset(second_plane[:], 0)
         one = keep.tile([P, 1], F32, name="one")
-        nc.scalar.activation(one[:], sums[:, GROUPS : GROUPS + 1], SQUARE, scale=1.0 / N)
+        nc.scalar.activation(one[:], sums[:, GROUPS - 1 : GROUPS], INV_SQRT, scale=1.0 / N)
 
         picked_scales = keep.tile([P, N], U8, name="picked_scales", align_bytes=64)
         nc.vector.tensor_copy(picked_scales[:], scale_pool[:].bitcast(U8).indirect(offsets[:]))
@@ -84,15 +85,22 @@ def tile_attend_nrm_taylor_topk_kernel(tc, qT, k_words, k_scales, offs, out):
 
         queries = [quantize_queries(0, q_first)]
 
-        picked_words = keep.tile([P, N], U32, name="picked_words", align_bytes=64)
-        nc.vector.tensor_copy(picked_words[:], word_pool[:].bitcast(U32).indirect(offsets[:]))
-        word_halves = picked_words[:].bitcast(U16).rearrange("p (n o) -> p o n", o=PASSES)
-        keys = []
-        for o in range(PASSES):
+        word_halves = []
+        for h in range(2):
+            picked = keep.tile([P, HALF], U32, name=f"picked_words{h}", align_bytes=64)
+            cols = slice(h * HALF // 16, (h + 1) * HALF // 16)
+            nc.vector.tensor_copy(picked[:], word_pool[:].bitcast(U32).indirect(offsets[:, cols]))
+            word_halves.append(picked[:].bitcast(U16).rearrange("p (n o) -> p o n", o=PASSES))
+
+        def part_words(o):
             parted = keep.tile([P, 2 * N], U8, name=f"keys{o}", align_bytes=64)
-            nc.vector.tensor_copy(parted[:].bitcast(U16), word_halves[:, o, :])
-            keys.append(parted)
+            for h in range(2):
+                nc.vector.tensor_copy(parted[:].bitcast(U16)[:, h * HALF : (h + 1) * HALF], word_halves[h][:, o, :])
+            return parted
+
+        keys = [part_words(0)]
         queries.append(quantize_queries(1, q_second))
+        keys.append(part_words(1))
 
         squares = keep.tile([P, N], F32, name="squares", align_bytes=64)
         banks = [psum.tile([P, GROUP], F32, name=f"scores{g}") for g in range(GROUPS)]
@@ -107,17 +115,22 @@ def tile_attend_nrm_taylor_topk_kernel(tc, qT, k_words, k_scales, offs, out):
                     start=(o == 0),
                     stop=(o == PASSES - 1),
                 )
+        last_sum = keep.tile([P, 1], F32, name="last_sum")
         for g in range(GROUPS):
+            total = sums[:, g : g + 1] if g < GROUPS - 1 else last_sum[:]
             nc.scalar.activation(
-                squares[:, g * GROUP : (g + 1) * GROUP], banks[g][:], SQUARE, bias=one[:], accum_out=sums[:, g : g + 1]
+                squares[:, g * GROUP : (g + 1) * GROUP], banks[g][:], SQUARE, bias=one[:], accum_out=total
             )
 
-        denom = keep.tile([P, 1], F32, name="denom")
-        nc.vector.tensor_reduce(denom[:], sums[:], mybir.AxisListType.X, ADD)
-        inverse = keep.tile([P, 1], F32, name="inverse")
-        nc.vector.reciprocal(inverse[:], denom[:])
+        numerators = keep.tile([P, N], F32, name="numerators", align_bytes=64)
+        nc.vector.tensor_scalar_add(numerators[:, :HALF], squares[:, :HALF], 1.0)
+        early_sum = keep.tile([P, 1], F32, name="early_sum")
+        nc.vector.tensor_reduce(early_sum[:], sums[:], mybir.AxisListType.X, ADD)
+        nc.vector.tensor_scalar_add(numerators[:, HALF:], squares[:, HALF:], 1.0)
+        root = keep.tile([P, 1], F32, name="root")
+        nc.scalar.activation(root[:], last_sum[:], INV_SQRT, bias=early_sum[:])
         for h, queue in enumerate((nc.sync, nc.scalar)):
             cols = slice(h * HALF, (h + 1) * HALF)
             weights = keep.tile([P, HALF], F32, name=f"weights{h}", align_bytes=64)
-            nc.vector.tensor_scalar(weights[:], squares[:, cols], 1.0, inverse[:], ADD, MULT)
+            nc.vector.tensor_scalar(weights[:], numerators[:, cols], root[:], root[:], MULT, MULT)
             queue.dma_start(out[0, :, cols], weights[:])

@@ -23,6 +23,8 @@ PASSES = D // K_PASS
 HALF = N // 2
 GROUP = 128
 GROUPS = N // GROUP
+SCALE_ROW0 = 96
+RAW_BYTES = PACK * NQ * 4
 
 FLOPS = 2 * NQ * N * D
 
@@ -31,44 +33,39 @@ def tile_attend_nrm_taylor_topk_kernel(tc, qT, k_words, k_scales, offs, out):
     nc = tc.nc
     with ExitStack() as ctx:
         keep = ctx.enter_context(tc.tile_pool(name="keep", bufs=1))
-        late = ctx.enter_context(tc.tile_pool(name="late", bufs=1))
+        shared = ctx.enter_context(tc.tile_pool(name="shared", bufs=1))
         psum = ctx.enter_context(tc.psum_pool(name="psum", bufs=1))
 
-        def load_queries(o, raw):
-            rows = qT[0, o * K_PASS : (o + 1) * K_PASS, :]
-            nc.sync.dma_start(raw[:], rows.rearrange("(p j) w -> p j w", j=PACK))
-
-        q_first = keep.tile([P, PACK, NQ], F32, name="q_first", align_bytes=64)
-        load_queries(0, q_first)
-
+        scale_pool = keep.tile([P, T // 4], I32, name="scale_pool", align_bytes=64)
+        nc.sync.dma_start(scale_pool[SCALE_ROW0:P, :], k_scales.bitcast(I32).rearrange("o f t -> f o t"))
         offsets = keep.tile([P, N // 16], U16, name="offsets")
         nc.sync.dma_start(offsets[:], offs)
-
-        scale_pool = keep.tile([P, T // 4], I32, name="scale_pool", align_bytes=64)
-        nc.vector.memset(scale_pool[:], 0)
-        scale_rows = k_scales.bitcast(I32).rearrange("o (b r) t -> r b o t", r=4)
-        for r in range(4):
-            nc.sync.dma_start(scale_pool[r:P:16, :], scale_rows[r])
-        shares = late.tile([P, 16], F32, name="shares", offset=4 * T - 32)
-        nc.vector.memset(shares[:], N / 16)
-        sums = keep.tile([P, GROUPS], F32, name="sums")
-        nc.vector.tensor_reduce(sums[:, GROUPS - 1 : GROUPS], shares[:], mybir.AxisListType.X, ADD)
-
-        word_pool = late.tile([P, T], I32, name="word_pool", offset=0, align_bytes=64)
+        word_pool = keep.tile([P, T], I32, name="word_pool", align_bytes=64)
         nc.sync.dma_start(word_pool[:], k_words[0].rearrange("p t b -> p (t b)").bitcast(I32))
-        q_second = late.tile([P, PACK, NQ], F32, name="q_second", offset=4 * T, align_bytes=64)
-        load_queries(1, q_second)
+        raws = []
+        for o in range(PASSES):
+            raw = shared.tile([P, PACK, NQ], F32, name=f"q_raw{o}", offset=o * RAW_BYTES, align_bytes=64)
+            rows = qT[0, o * K_PASS : (o + 1) * K_PASS, :]
+            nc.sync.dma_start(raw[:], rows.rearrange("(p j) w -> p j w", j=PACK))
+            raws.append(raw)
+        q_first, q_second = raws
 
-        second_plane = keep.tile([P, N // 4], I32, name="second_plane", align_bytes=64)
-        nc.vector.memset(second_plane[:], 0)
+        nc.vector.memset(scale_pool[0:SCALE_ROW0, :], 0)
+        both_planes = keep.tile([P, PASSES, N // 4], I32, name="both_planes", align_bytes=64)
+        nc.vector.memset(both_planes[:], 0)
+        sums = keep.tile([P, GROUPS], F32, name="sums")
+        nc.vector.memset(sums[:, GROUPS - 1 : GROUPS], float(N))
         one = keep.tile([P, 1], F32, name="one")
         nc.scalar.activation(one[:], sums[:, GROUPS - 1 : GROUPS], INV_SQRT, scale=1.0 / N)
 
         picked_scales = keep.tile([P, N], U8, name="picked_scales", align_bytes=64)
         nc.vector.tensor_copy(picked_scales[:], scale_pool[:].bitcast(U8).indirect(offsets[:]))
-        for r in range(4):
-            nc.sync.dma_start(second_plane[r:P:32, :], picked_scales[:].bitcast(I32)[16 + r : P : 32, :])
-        planes = [picked_scales[:], second_plane[:].bitcast(U8)]
+        for quad in range(4):
+            first = SCALE_ROW0 + 8 * quad
+            nc.sync.dma_start(
+                both_planes[32 * quad : 32 * quad + 4, :, :], picked_scales[:].bitcast(I32)[first : first + 8, :]
+            )
+        planes = [both_planes[:, o, :].bitcast(U8) for o in range(PASSES)]
 
         def quantize_queries(o, raw):
             grouped = keep.tile([P, NQ, PACK], BF16, name=f"q_grouped{o}", align_bytes=64)
@@ -83,8 +80,6 @@ def tile_attend_nrm_taylor_topk_kernel(tc, qT, k_words, k_scales, offs, out):
             )
             return codes, scales
 
-        queries = [quantize_queries(0, q_first)]
-
         word_halves = []
         for h in range(2):
             picked = keep.tile([P, HALF], U32, name=f"picked_words{h}", align_bytes=64)
@@ -92,15 +87,15 @@ def tile_attend_nrm_taylor_topk_kernel(tc, qT, k_words, k_scales, offs, out):
             nc.vector.tensor_copy(picked[:], word_pool[:].bitcast(U32).indirect(offsets[:, cols]))
             word_halves.append(picked[:].bitcast(U16).rearrange("p (n o) -> p o n", o=PASSES))
 
-        def part_words(o):
-            parted = keep.tile([P, 2 * N], U8, name=f"keys{o}", align_bytes=64)
+        def part_words(o, parted):
             for h in range(2):
                 nc.vector.tensor_copy(parted[:].bitcast(U16)[:, h * HALF : (h + 1) * HALF], word_halves[h][:, o, :])
             return parted
 
-        keys = [part_words(0)]
+        keys = [part_words(0, keep.tile([P, 2 * N], U8, name="keys0", align_bytes=64))]
+        queries = [quantize_queries(0, q_first)]
+        keys.append(part_words(1, shared.tile([P, 2 * N], U8, name="keys1", offset=0, align_bytes=64)))
         queries.append(quantize_queries(1, q_second))
-        keys.append(part_words(1))
 
         squares = keep.tile([P, N], F32, name="squares", align_bytes=64)
         banks = [psum.tile([P, GROUP], F32, name=f"scores{g}") for g in range(GROUPS)]

@@ -10,9 +10,9 @@ U16 = mybir.dt.uint16
 U8 = mybir.dt.uint8
 FP8X4 = mybir.dt.float8_e4m3fn_x4
 FP4X4 = mybir.dt.float4_e2m1fn_x4
-ADD = mybir.AluOpType.add
 MULT = mybir.AluOpType.mult
 SQUARE = mybir.ActivationFunctionType.Square
+COPY = mybir.ActivationFunctionType.Copy
 INV_SQRT = mybir.ActivationFunctionType.Abs_reciprocal_sqrt
 
 P = 128
@@ -62,7 +62,7 @@ def tile_attend_nrm_taylor_topk_kernel(tc, qT, k_words, k_scales, offs, out):
         nc.vector.tensor_copy(picked_scales[:], scale_pool[:].bitcast(U8).indirect(offsets[:]))
         for quad in range(4):
             first = SCALE_ROW0 + 8 * quad
-            nc.sync.dma_start(
+            (nc.sync, nc.scalar)[quad % 2].dma_start(
                 both_planes[32 * quad : 32 * quad + 4, :, :], picked_scales[:].bitcast(I32)[first : first + 8, :]
             )
         planes = [both_planes[:, o, :].bitcast(U8) for o in range(PASSES)]
@@ -87,15 +87,19 @@ def tile_attend_nrm_taylor_topk_kernel(tc, qT, k_words, k_scales, offs, out):
             nc.vector.tensor_copy(picked[:], word_pool[:].bitcast(U32).indirect(offsets[:, cols]))
             word_halves.append(picked[:].bitcast(U16).rearrange("p (n o) -> p o n", o=PASSES))
 
-        def part_words(o, parted):
-            for h in range(2):
-                nc.vector.tensor_copy(parted[:].bitcast(U16)[:, h * HALF : (h + 1) * HALF], word_halves[h][:, o, :])
+        def part_words(o, h, parted):
+            nc.vector.tensor_copy(parted[:].bitcast(U16), word_halves[h][:, o, :])
             return parted
 
-        keys = [part_words(0, keep.tile([P, 2 * N], U8, name="keys0", align_bytes=64))]
+        def late_keys(name, offset):
+            return shared.tile([P, 2 * HALF], U8, name=name, offset=offset, align_bytes=64)
+
+        keys = {(0, 0): part_words(0, 0, keep.tile([P, 2 * HALF], U8, name="keys00", align_bytes=64))}
         queries = [quantize_queries(0, q_first)]
-        keys.append(part_words(1, shared.tile([P, 2 * N], U8, name="keys1", offset=0, align_bytes=64)))
+        keys[0, 1] = part_words(0, 1, late_keys("keys01", 0))
+        keys[1, 0] = part_words(1, 0, late_keys("keys10", 2 * HALF))
         queries.append(quantize_queries(1, q_second))
+        keys[1, 1] = part_words(1, 1, late_keys("keys11", RAW_BYTES))
 
         squares = keep.tile([P, N], F32, name="squares", align_bytes=64)
         banks = [psum.tile([P, GROUP], F32, name=f"scores{g}") for g in range(GROUPS)]
@@ -105,7 +109,7 @@ def tile_attend_nrm_taylor_topk_kernel(tc, qT, k_words, k_scales, offs, out):
                     out=banks[g][:],
                     lhsT=queries[o][0][:].bitcast(FP8X4),
                     lhsT_scale=queries[o][1][:],
-                    rhs=keys[o][:, 2 * g * GROUP : 2 * (g + 1) * GROUP].bitcast(FP4X4),
+                    rhs=keys[o, g // 2][:, 2 * (g % 2) * GROUP : 2 * (g % 2 + 1) * GROUP].bitcast(FP4X4),
                     rhs_scale=planes[o][:, g * GROUP : (g + 1) * GROUP],
                     start=(o == 0),
                     stop=(o == PASSES - 1),
@@ -120,7 +124,8 @@ def tile_attend_nrm_taylor_topk_kernel(tc, qT, k_words, k_scales, offs, out):
         numerators = keep.tile([P, N], F32, name="numerators", align_bytes=64)
         nc.vector.tensor_scalar_add(numerators[:, :HALF], squares[:, :HALF], 1.0)
         early_sum = keep.tile([P, 1], F32, name="early_sum")
-        nc.vector.tensor_reduce(early_sum[:], sums[:], mybir.AxisListType.X, ADD)
+        sums_again = keep.tile([P, GROUPS], F32, name="sums_again")
+        nc.scalar.activation(sums_again[:], sums[:], COPY, accum_out=early_sum[:])
         nc.vector.tensor_scalar_add(numerators[:, HALF:], squares[:, HALF:], 1.0)
         root = keep.tile([P, 1], F32, name="root")
         nc.scalar.activation(root[:], last_sum[:], INV_SQRT, bias=early_sum[:])

@@ -24,6 +24,7 @@ HALF = N // 2
 GROUP = 128
 GROUPS = N // GROUP
 SCALE_ROW0 = 96
+SCALAR_COLS = 96
 RAW_BYTES = PACK * NQ * 4
 
 FLOPS = 2 * NQ * N * D
@@ -48,15 +49,14 @@ def tile_attend_nrm_taylor_topk_kernel(tc, qT, k_words, k_scales, offs, out):
             rows = qT[0, o * K_PASS : (o + 1) * K_PASS, :]
             nc.sync.dma_start(raw[:], rows.rearrange("(p j) w -> p j w", j=PACK))
             raws.append(raw)
-        q_first, q_second = raws
 
         nc.vector.memset(scale_pool[0:SCALE_ROW0, :], 0)
         both_planes = keep.tile([P, PASSES, N // 4], I32, name="both_planes", align_bytes=64)
         nc.vector.memset(both_planes[:], 0)
         sums = keep.tile([P, GROUPS], F32, name="sums")
-        nc.vector.memset(sums[:, GROUPS - 1 : GROUPS], float(N))
         one = keep.tile([P, 1], F32, name="one")
-        nc.scalar.activation(one[:], sums[:, GROUPS - 1 : GROUPS], INV_SQRT, scale=1.0 / N)
+        nc.vector.memset(one[:], 1.0)
+        nc.scalar.activation(sums[:, GROUPS - 1 : GROUPS], one[:], INV_SQRT, scale=1.0 / N**2)
 
         picked_scales = keep.tile([P, N], U8, name="picked_scales", align_bytes=64)
         nc.vector.tensor_copy(picked_scales[:], scale_pool[:].bitcast(U8).indirect(offsets[:]))
@@ -67,58 +67,79 @@ def tile_attend_nrm_taylor_topk_kernel(tc, qT, k_words, k_scales, offs, out):
             )
         planes = [both_planes[:, o, :].bitcast(U8) for o in range(PASSES)]
 
-        def quantize_queries(o, raw):
-            grouped = keep.tile([P, NQ, PACK], BF16, name=f"q_grouped{o}", align_bytes=64)
-            nc.scalar.copy(
-                grouped[:].rearrange("p (c i) t -> p c t i", i=4),
-                raw[:].rearrange("p t (c i) -> p c t i", i=4),
+        def round_queries(copy, o, cols):
+            copy(
+                groupeds[o][:, cols, :].rearrange("p (c i) t -> p c t i", i=4),
+                raws[o][:, :, cols].rearrange("p t (c i) -> p c t i", i=4),
             )
+
+        def quantize_queries(o):
             codes = keep.tile([P, NQ], U32, name=f"q_codes{o}", align_bytes=64)
             scales = keep.tile([P, NQ], U8, name=f"q_scales{o}", align_bytes=64)
             nc.vector.quantize_mx(
-                out=codes[:].bitcast(FP8X4), scales=scales[:], in_=grouped[:].rearrange("p w j -> p (w j)")
+                out=codes[:].bitcast(FP8X4), scales=scales[:], in_=groupeds[o][:].rearrange("p w j -> p (w j)")
             )
             return codes, scales
 
-        word_halves = []
+        groupeds = [keep.tile([P, NQ, PACK], BF16, name=f"q_grouped{o}", align_bytes=64) for o in range(PASSES)]
+        round_queries(nc.scalar.copy, 0, slice(0, NQ))
+        round_queries(nc.scalar.copy, 1, slice(0, SCALAR_COLS))
+
+        picked = []
         for h in range(2):
-            picked = keep.tile([P, HALF], U32, name=f"picked_words{h}", align_bytes=64)
+            words = keep.tile([P, HALF], U32, name=f"picked_words{h}", align_bytes=64)
             cols = slice(h * HALF // 16, (h + 1) * HALF // 16)
-            nc.vector.tensor_copy(picked[:], word_pool[:].bitcast(U32).indirect(offsets[:, cols]))
-            word_halves.append(picked[:].bitcast(U16).rearrange("p (n o) -> p o n", o=PASSES))
+            nc.vector.tensor_copy(words[:], word_pool[:].bitcast(U32).indirect(offsets[:, cols]))
+            picked.append(words[:].bitcast(U16).rearrange("p (g n o) -> p g o n", g=2, o=PASSES))
 
-        def part_words(o, h, parted):
-            nc.vector.tensor_copy(parted[:].bitcast(U16), word_halves[h][:, o, :])
-            return parted
+        keys = {}
 
-        def late_keys(name, offset):
-            return shared.tile([P, 2 * HALF], U8, name=name, offset=offset, align_bytes=64)
+        def part_pass(o, groups, tile):
+            h, g0 = divmod(groups[0], 2)
+            nc.vector.tensor_copy(
+                tile[:].bitcast(U16).rearrange("p (g n) -> p g n", n=GROUP), picked[h][:, g0 : g0 + len(groups), o, :]
+            )
+            for i, g in enumerate(groups):
+                keys[o, g] = tile[:, 2 * i * GROUP : 2 * (i + 1) * GROUP]
 
-        keys = {(0, 0): part_words(0, 0, keep.tile([P, 2 * HALF], U8, name="keys00", align_bytes=64))}
-        queries = [quantize_queries(0, q_first)]
-        keys[0, 1] = part_words(0, 1, late_keys("keys01", 0))
-        keys[1, 0] = part_words(1, 0, late_keys("keys10", 2 * HALF))
-        queries.append(quantize_queries(1, q_second))
-        keys[1, 1] = part_words(1, 1, late_keys("keys11", RAW_BYTES))
+        def part_group(g, tile):
+            nc.vector.tensor_copy(
+                tile[:].bitcast(U16).rearrange("p (o n) -> p o n", n=GROUP), picked[g // 2][:, g % 2, :, :]
+            )
+            for o in range(PASSES):
+                keys[o, g] = tile[:, 2 * o * GROUP : 2 * (o + 1) * GROUP]
+
+        def late_tile(name, units, offset):
+            return shared.tile([P, 2 * GROUP * units], U8, name=name, offset=offset, align_bytes=64)
+
+        part_pass(0, (0, 1), keep.tile([P, 4 * GROUP], U8, name="keys_a", align_bytes=64))
+        round_queries(nc.vector.tensor_copy, 1, slice(SCALAR_COLS, NQ))
+        queries = [quantize_queries(0)]
+        part_pass(0, (2,), late_tile("keys_b", 1, 0))
+        queries.append(quantize_queries(1))
+        for g in range(GROUPS - 1):
+            part_pass(1, (g,), late_tile(f"keys_c{g}", 1, RAW_BYTES + 2 * GROUP * g))
+        part_group(3, late_tile("keys_e", 2, RAW_BYTES + 6 * GROUP))
 
         squares = keep.tile([P, N], F32, name="squares", align_bytes=64)
         banks = [psum.tile([P, GROUP], F32, name=f"scores{g}") for g in range(GROUPS)]
-        for o in range(PASSES):
-            for g in range(GROUPS):
-                nc.tensor.matmul_mx(
-                    out=banks[g][:],
-                    lhsT=queries[o][0][:].bitcast(FP8X4),
-                    lhsT_scale=queries[o][1][:],
-                    rhs=keys[o, g // 2][:, 2 * (g % 2) * GROUP : 2 * (g % 2 + 1) * GROUP].bitcast(FP4X4),
-                    rhs_scale=planes[o][:, g * GROUP : (g + 1) * GROUP],
-                    start=(o == 0),
-                    stop=(o == PASSES - 1),
-                )
+        for groups in (range(GROUPS - 1), range(GROUPS - 1, GROUPS)):
+            for o in range(PASSES):
+                for g in groups:
+                    nc.tensor.matmul_mx(
+                        out=banks[g][:],
+                        lhsT=queries[o][0][:].bitcast(FP8X4),
+                        lhsT_scale=queries[o][1][:],
+                        rhs=keys[o, g].bitcast(FP4X4),
+                        rhs_scale=planes[o][:, g * GROUP : (g + 1) * GROUP],
+                        start=(o == 0),
+                        stop=(o == PASSES - 1),
+                    )
         last_sum = keep.tile([P, 1], F32, name="last_sum")
         for g in range(GROUPS):
             total = sums[:, g : g + 1] if g < GROUPS - 1 else last_sum[:]
             nc.scalar.activation(
-                squares[:, g * GROUP : (g + 1) * GROUP], banks[g][:], SQUARE, bias=one[:], accum_out=total
+                squares[:, g * GROUP : (g + 1) * GROUP], banks[g][:], SQUARE, bias=1.0, accum_out=total
             )
 
         numerators = keep.tile([P, N], F32, name="numerators", align_bytes=64)

@@ -116,9 +116,9 @@ def tile_attend_nrm_taylor_topk_kernel(tc, qT, k_words, k_scales, offs, out):
         round_queries(nc.vector.tensor_copy, 1, slice(SCALAR_COLS, NQ))
         queries = [quantize_queries(0)]
         part_pass(0, (2,), late_tile("keys_b", 1, 0))
+        part_pass(1, (0, 1), late_tile("keys_c", 2, 2 * GROUP))
         queries.append(quantize_queries(1))
-        for g in range(GROUPS - 1):
-            part_pass(1, (g,), late_tile(f"keys_c{g}", 1, RAW_BYTES + 2 * GROUP * g))
+        part_pass(1, (2,), late_tile("keys_d", 1, RAW_BYTES))
         part_group(3, late_tile("keys_e", 2, RAW_BYTES + 6 * GROUP))
 
         squares = keep.tile([P, N], F32, name="squares", align_bytes=64)

@@ -150,8 +150,6 @@ def tile_attend_nrm_taylor_topk_kernel(tc, qT, k_words, k_scales, offs, out):
         nc.vector.tensor_scalar_add(numerators[:, HALF:], squares[:, HALF:], 1.0)
         root = keep.tile([P, 1], F32, name="root")
         nc.scalar.activation(root[:], last_sum[:], INV_SQRT, bias=early_sum[:])
-        for h, queue in enumerate((nc.sync, nc.scalar)):
-            cols = slice(h * HALF, (h + 1) * HALF)
-            weights = keep.tile([P, HALF], F32, name=f"weights{h}", align_bytes=64)
-            nc.vector.tensor_scalar(weights[:], numerators[:, cols], root[:], root[:], MULT, MULT)
-            queue.dma_start(out[0, :, cols], weights[:])
+        weights = keep.tile([P, N], F32, name="weights", align_bytes=64)
+        nc.vector.tensor_scalar(weights[:], numerators[:], root[:], root[:], MULT, MULT)
+        nc.sync.dma_start(out[0], weights[:])

@@ -147,9 +147,12 @@ def tile_attend_nrm_taylor_topk_kernel(tc, qT, k_words, k_scales, offs, out):
         early_sum = keep.tile([P, 1], F32, name="early_sum")
         sums_again = keep.tile([P, GROUPS], F32, name="sums_again")
         nc.scalar.activation(sums_again[:], sums[:], COPY, accum_out=early_sum[:])
-        nc.vector.tensor_scalar_add(numerators[:, HALF:], squares[:, HALF:], 1.0)
+        for g in range(2, GROUPS):
+            cols = slice(g * GROUP, (g + 1) * GROUP)
+            nc.vector.tensor_scalar_add(numerators[:, cols], squares[:, cols], 1.0)
         root = keep.tile([P, 1], F32, name="root")
         nc.scalar.activation(root[:], last_sum[:], INV_SQRT, bias=early_sum[:])
         weights = keep.tile([P, N], F32, name="weights", align_bytes=64)
-        nc.vector.tensor_scalar(weights[:], numerators[:], root[:], root[:], MULT, MULT)
+        for cols in (slice(0, N - GROUP), slice(N - GROUP, N)):
+            nc.vector.tensor_scalar(weights[:, cols], numerators[:, cols], root[:], root[:], MULT, MULT)
         nc.sync.dma_start(out[0], weights[:])

@@ -26,6 +26,7 @@ GROUPS = N // GROUP
 SCALE_ROW0 = 96
 SCALAR_COLS = 96
 RAW_BYTES = PACK * NQ * 4
+DMA_ALIGN = 256
 
 FLOPS = 2 * NQ * N * D
 
@@ -37,28 +38,28 @@ def tile_attend_nrm_taylor_topk_kernel(tc, qT, k_words, k_scales, offs, out):
         shared = ctx.enter_context(tc.tile_pool(name="shared", bufs=1))
         psum = ctx.enter_context(tc.psum_pool(name="psum", bufs=1))
 
-        scale_pool = keep.tile([P, T // 4], I32, name="scale_pool", align_bytes=64)
+        scale_pool = keep.tile([P, T // 4], I32, name="scale_pool", align_bytes=DMA_ALIGN)
         nc.sync.dma_start(scale_pool[SCALE_ROW0:P, :], k_scales.bitcast(I32).rearrange("o f t -> f o t"))
         offsets = keep.tile([P, N // 16], U16, name="offsets")
         nc.sync.dma_start(offsets[:], offs)
-        word_pool = keep.tile([P, T], I32, name="word_pool", align_bytes=64)
+        word_pool = keep.tile([P, T], I32, name="word_pool", align_bytes=DMA_ALIGN)
         nc.sync.dma_start(word_pool[:], k_words[0].rearrange("p t b -> p (t b)").bitcast(I32))
         raws = []
         for o in range(PASSES):
-            raw = shared.tile([P, PACK, NQ], F32, name=f"q_raw{o}", offset=o * RAW_BYTES, align_bytes=64)
+            raw = shared.tile([P, PACK, NQ], F32, name=f"q_raw{o}", offset=o * RAW_BYTES, align_bytes=DMA_ALIGN)
             rows = qT[0, o * K_PASS : (o + 1) * K_PASS, :]
             nc.sync.dma_start(raw[:], rows.rearrange("(p j) w -> p j w", j=PACK))
             raws.append(raw)
 
         nc.vector.memset(scale_pool[0:SCALE_ROW0, :], 0)
-        both_planes = keep.tile([P, PASSES, N // 4], I32, name="both_planes", align_bytes=64)
+        both_planes = keep.tile([P, PASSES, N // 4], I32, name="both_planes", align_bytes=DMA_ALIGN)
         nc.vector.memset(both_planes[:], 0)
         sums = keep.tile([P, GROUPS], F32, name="sums")
         one = keep.tile([P, 1], F32, name="one")
         nc.vector.memset(one[:], 1.0)
         nc.scalar.activation(sums[:, GROUPS - 1 : GROUPS], one[:], INV_SQRT, scale=1.0 / N**2)
 
-        picked_scales = keep.tile([P, N], U8, name="picked_scales", align_bytes=64)
+        picked_scales = keep.tile([P, N], U8, name="picked_scales", align_bytes=DMA_ALIGN)
         nc.vector.tensor_copy(picked_scales[:], scale_pool[:].bitcast(U8).indirect(offsets[:]))
         for quad in range(4):
             first = SCALE_ROW0 + 8 * quad
@@ -152,7 +153,7 @@ def tile_attend_nrm_taylor_topk_kernel(tc, qT, k_words, k_scales, offs, out):
             nc.vector.tensor_scalar_add(numerators[:, cols], squares[:, cols], 1.0)
         root = keep.tile([P, 1], F32, name="root")
         nc.scalar.activation(root[:], last_sum[:], INV_SQRT, bias=early_sum[:])
-        weights = keep.tile([P, N], F32, name="weights", align_bytes=64)
+        weights = keep.tile([P, N], F32, name="weights", align_bytes=DMA_ALIGN)
         for cols in (slice(0, N - GROUP), slice(N - GROUP, N)):
             nc.vector.tensor_scalar(weights[:, cols], numerators[:, cols], root[:], root[:], MULT, MULT)
         nc.sync.dma_start(out[0], weights[:])

@@ -26,7 +26,7 @@ GROUPS = N // GROUP
 SCALE_ROW0 = 96
 SCALAR_COLS = 96
 RAW_BYTES = PACK * NQ * 4
-DMA_ALIGN = 256
+ALIGN = 256
 
 FLOPS = 2 * NQ * N * D
 
@@ -38,28 +38,28 @@ def tile_attend_nrm_taylor_topk_kernel(tc, qT, k_words, k_scales, offs, out):
         shared = ctx.enter_context(tc.tile_pool(name="shared", bufs=1))
         psum = ctx.enter_context(tc.psum_pool(name="psum", bufs=1))
 
-        scale_pool = keep.tile([P, T // 4], I32, name="scale_pool", align_bytes=DMA_ALIGN)
+        scale_pool = keep.tile([P, T // 4], I32, name="scale_pool", align_bytes=ALIGN)
         nc.sync.dma_start(scale_pool[SCALE_ROW0:P, :], k_scales.bitcast(I32).rearrange("o f t -> f o t"))
         offsets = keep.tile([P, N // 16], U16, name="offsets")
         nc.sync.dma_start(offsets[:], offs)
-        word_pool = keep.tile([P, T], I32, name="word_pool", align_bytes=DMA_ALIGN)
+        word_pool = keep.tile([P, T], I32, name="word_pool", align_bytes=ALIGN)
         nc.sync.dma_start(word_pool[:], k_words[0].rearrange("p t b -> p (t b)").bitcast(I32))
         raws = []
         for o in range(PASSES):
-            raw = shared.tile([P, PACK, NQ], F32, name=f"q_raw{o}", offset=o * RAW_BYTES, align_bytes=DMA_ALIGN)
+            raw = shared.tile([P, PACK, NQ], F32, name=f"q_raw{o}", offset=o * RAW_BYTES, align_bytes=ALIGN)
             rows = qT[0, o * K_PASS : (o + 1) * K_PASS, :]
             nc.sync.dma_start(raw[:], rows.rearrange("(p j) w -> p j w", j=PACK))
             raws.append(raw)
 
         nc.vector.memset(scale_pool[0:SCALE_ROW0, :], 0)
-        both_planes = keep.tile([P, PASSES, N // 4], I32, name="both_planes", align_bytes=DMA_ALIGN)
+        both_planes = keep.tile([P, PASSES, N // 4], I32, name="both_planes", align_bytes=ALIGN)
         nc.vector.memset(both_planes[:], 0)
         sums = keep.tile([P, GROUPS], F32, name="sums")
         one = keep.tile([P, 1], F32, name="one")
         nc.vector.memset(one[:], 1.0)
         nc.scalar.activation(sums[:, GROUPS - 1 : GROUPS], one[:], INV_SQRT, scale=1.0 / N**2)
 
-        picked_scales = keep.tile([P, N], U8, name="picked_scales", align_bytes=DMA_ALIGN)
+        picked_scales = keep.tile([P, N], U8, name="picked_scales", align_bytes=ALIGN)
         nc.vector.tensor_copy(picked_scales[:], scale_pool[:].bitcast(U8).indirect(offsets[:]))
         for quad in range(4):
             first = SCALE_ROW0 + 8 * quad
@@ -75,20 +75,20 @@ def tile_attend_nrm_taylor_topk_kernel(tc, qT, k_words, k_scales, offs, out):
             )
 
         def quantize_queries(o):
-            codes = keep.tile([P, NQ], U32, name=f"q_codes{o}", align_bytes=64)
-            scales = keep.tile([P, NQ], U8, name=f"q_scales{o}", align_bytes=64)
+            codes = keep.tile([P, NQ], U32, name=f"q_codes{o}", align_bytes=ALIGN)
+            scales = keep.tile([P, NQ], U8, name=f"q_scales{o}", align_bytes=ALIGN)
             nc.vector.quantize_mx(
                 out=codes[:].bitcast(FP8X4), scales=scales[:], in_=groupeds[o][:].rearrange("p w j -> p (w j)")
             )
             return codes, scales
 
-        groupeds = [keep.tile([P, NQ, PACK], BF16, name=f"q_grouped{o}", align_bytes=64) for o in range(PASSES)]
+        groupeds = [keep.tile([P, NQ, PACK], BF16, name=f"q_grouped{o}", align_bytes=ALIGN) for o in range(PASSES)]
         round_queries(nc.scalar.copy, 0, slice(0, NQ))
         round_queries(nc.scalar.copy, 1, slice(0, SCALAR_COLS))
 
         picked = []
         for h in range(2):
-            words = keep.tile([P, HALF], U32, name=f"picked_words{h}", align_bytes=64)
+            words = keep.tile([P, HALF], U32, name=f"picked_words{h}", align_bytes=ALIGN)
             cols = slice(h * HALF // 16, (h + 1) * HALF // 16)
             nc.vector.tensor_copy(words[:], word_pool[:].bitcast(U32).indirect(offsets[:, cols]))
             picked.append(words[:].bitcast(U16).rearrange("p (g n o) -> p g o n", g=2, o=PASSES))
@@ -111,9 +111,9 @@ def tile_attend_nrm_taylor_topk_kernel(tc, qT, k_words, k_scales, offs, out):
                 keys[o, g] = tile[:, 2 * o * GROUP : 2 * (o + 1) * GROUP]
 
         def late_tile(name, units, offset):
-            return shared.tile([P, 2 * GROUP * units], U8, name=name, offset=offset, align_bytes=64)
+            return shared.tile([P, 2 * GROUP * units], U8, name=name, offset=offset, align_bytes=ALIGN)
 
-        part_pass(0, (0, 1), keep.tile([P, 4 * GROUP], U8, name="keys_a", align_bytes=64))
+        part_pass(0, (0, 1), keep.tile([P, 4 * GROUP], U8, name="keys_a", align_bytes=ALIGN))
         round_queries(nc.vector.tensor_copy, 1, slice(SCALAR_COLS, NQ))
         queries = [quantize_queries(0)]
         part_pass(0, (2,), late_tile("keys_b", 1, 0))
@@ -122,7 +122,7 @@ def tile_attend_nrm_taylor_topk_kernel(tc, qT, k_words, k_scales, offs, out):
         part_pass(1, (2,), late_tile("keys_d", 1, RAW_BYTES))
         part_group(3, late_tile("keys_e", 2, RAW_BYTES + 6 * GROUP))
 
-        squares = keep.tile([P, N], F32, name="squares", align_bytes=64)
+        squares = keep.tile([P, N], F32, name="squares", align_bytes=ALIGN)
         banks = [psum.tile([P, GROUP], F32, name=f"scores{g}") for g in range(GROUPS)]
         for groups in (range(GROUPS - 1), range(GROUPS - 1, GROUPS)):
             for o in range(PASSES):
@@ -143,7 +143,7 @@ def tile_attend_nrm_taylor_topk_kernel(tc, qT, k_words, k_scales, offs, out):
                 squares[:, g * GROUP : (g + 1) * GROUP], banks[g][:], SQUARE, bias=1.0, accum_out=total
             )
 
-        numerators = keep.tile([P, N], F32, name="numerators", align_bytes=64)
+        numerators = keep.tile([P, N], F32, name="numerators", align_bytes=ALIGN)
         nc.vector.tensor_scalar_add(numerators[:, :HALF], squares[:, :HALF], 1.0)
         early_sum = keep.tile([P, 1], F32, name="early_sum")
         sums_again = keep.tile([P, GROUPS], F32, name="sums_again")
@@ -153,7 +153,7 @@ def tile_attend_nrm_taylor_topk_kernel(tc, qT, k_words, k_scales, offs, out):
             nc.vector.tensor_scalar_add(numerators[:, cols], squares[:, cols], 1.0)
         root = keep.tile([P, 1], F32, name="root")
         nc.scalar.activation(root[:], last_sum[:], INV_SQRT, bias=early_sum[:])
-        weights = keep.tile([P, N], F32, name="weights", align_bytes=DMA_ALIGN)
+        weights = keep.tile([P, N], F32, name="weights", align_bytes=ALIGN)
         for cols in (slice(0, N - GROUP), slice(N - GROUP, N)):
             nc.vector.tensor_scalar(weights[:, cols], numerators[:, cols], root[:], root[:], MULT, MULT)
         nc.sync.dma_start(out[0], weights[:])

@@ -70,8 +70,8 @@ def tile_attend_nrm_taylor_topk_kernel(tc, qT, k_words, k_scales, offs, out):
 
         def round_queries(copy, o, cols):
             copy(
-                groupeds[o][:, cols, :].rearrange("p (c i) t -> p c t i", i=4),
-                raws[o][:, :, cols].rearrange("p t (c i) -> p c t i", i=4),
+                groupeds[o][:, cols, :].rearrange("p (c i) t -> p c t i", i=2),
+                raws[o][:, :, cols].rearrange("p t (c i) -> p c t i", i=2),
             )
 
         def quantize_queries(o):

@@ -24,7 +24,7 @@ HALF = N // 2
 GROUP = 128
 GROUPS = N // GROUP
 SCALE_ROW0 = 96
-SCALAR_COLS = 96
+SCALAR_COLS = 88
 RAW_BYTES = PACK * NQ * 4
 ALIGN = 256
 
@@ -86,41 +86,39 @@ def tile_attend_nrm_taylor_topk_kernel(tc, qT, k_words, k_scales, offs, out):
         round_queries(nc.scalar.copy, 0, slice(0, NQ))
         round_queries(nc.scalar.copy, 1, slice(0, SCALAR_COLS))
 
-        picked = []
-        for h in range(2):
-            words = keep.tile([P, HALF], U32, name=f"picked_words{h}", align_bytes=ALIGN)
-            cols = slice(h * HALF // 16, (h + 1) * HALF // 16)
+        picked = {}
+        for groups in (range(1), range(1, GROUPS)):
+            words = keep.tile([P, len(groups) * GROUP], U32, name=f"picked_words{groups[0]}", align_bytes=ALIGN)
+            cols = slice(groups[0] * GROUP // 16, (groups[-1] + 1) * GROUP // 16)
             nc.vector.tensor_copy(words[:], word_pool[:].bitcast(U32).indirect(offsets[:, cols]))
-            picked.append(words[:].bitcast(U16).rearrange("p (g n o) -> p g o n", g=2, o=PASSES))
+            halves = words[:].bitcast(U16).rearrange("p (n o) -> p o n", o=PASSES)
+            for i, g in enumerate(groups):
+                picked[g] = halves[:, :, i * GROUP :]
 
         keys = {}
 
-        def part_pass(o, groups, tile):
-            h, g0 = divmod(groups[0], 2)
+        def part(passes, groups, tile):
+            width = len(groups) * GROUP
             nc.vector.tensor_copy(
-                tile[:].bitcast(U16).rearrange("p (g n) -> p g n", n=GROUP), picked[h][:, g0 : g0 + len(groups), o, :]
+                tile[:].bitcast(U16).rearrange("p (o n) -> p o n", n=width),
+                picked[groups[0]][:, passes[0] : passes[-1] + 1, :width],
             )
-            for i, g in enumerate(groups):
-                keys[o, g] = tile[:, 2 * i * GROUP : 2 * (i + 1) * GROUP]
-
-        def part_group(g, tile):
-            nc.vector.tensor_copy(
-                tile[:].bitcast(U16).rearrange("p (o n) -> p o n", n=GROUP), picked[g // 2][:, g % 2, :, :]
-            )
-            for o in range(PASSES):
-                keys[o, g] = tile[:, 2 * o * GROUP : 2 * (o + 1) * GROUP]
+            for i, o in enumerate(passes):
+                for j, g in enumerate(groups):
+                    at = 2 * (i * width + j * GROUP)
+                    keys[o, g] = tile[:, at : at + 2 * GROUP]
 
         def late_tile(name, units, offset):
             return shared.tile([P, 2 * GROUP * units], U8, name=name, offset=offset, align_bytes=ALIGN)
 
-        part_pass(0, (0, 1), keep.tile([P, 4 * GROUP], U8, name="keys_a", align_bytes=ALIGN))
+        part((0,), (0,), keep.tile([P, 2 * GROUP], U8, name="keys_a", align_bytes=ALIGN))
         round_queries(nc.vector.tensor_copy, 1, slice(SCALAR_COLS, NQ))
         queries = [quantize_queries(0)]
-        part_pass(0, (2,), late_tile("keys_b", 1, 0))
-        part_pass(1, (0, 1), late_tile("keys_c", 2, 2 * GROUP))
+        part((0,), (1, 2), late_tile("keys_b", 2, 0))
+        part((1,), (0,), late_tile("keys_c", 1, 4 * GROUP))
         queries.append(quantize_queries(1))
-        part_pass(1, (2,), late_tile("keys_d", 1, RAW_BYTES))
-        part_group(3, late_tile("keys_e", 2, RAW_BYTES + 6 * GROUP))
+        part((1,), (1, 2), late_tile("keys_d", 2, RAW_BYTES))
+        part((0, 1), (3,), late_tile("keys_e", 2, RAW_BYTES + 6 * GROUP))
 
         squares = keep.tile([P, N], F32, name="squares", align_bytes=ALIGN)
         banks = [psum.tile([P, GROUP], F32, name=f"scores{g}") for g in range(GROUPS)]

from contextlib import ExitStack

import concourse.mybir as mybir

F32 = mybir.dt.float32
BF16 = mybir.dt.bfloat16
I32 = mybir.dt.int32
U32 = mybir.dt.uint32
U16 = mybir.dt.uint16
U8 = mybir.dt.uint8
FP8X4 = mybir.dt.float8_e4m3fn_x4
FP4X4 = mybir.dt.float4_e2m1fn_x4
MULT = mybir.AluOpType.mult
SQUARE = mybir.ActivationFunctionType.Square
COPY = mybir.ActivationFunctionType.Copy
INV_SQRT = mybir.ActivationFunctionType.Abs_reciprocal_sqrt

P = 128
PACK = 4
K_PASS = P * PACK
D, T, N, NQ = 1024, 2048, 512, 128
PASSES = D // K_PASS
HALF = N // 2
GROUP = 128
GROUPS = N // GROUP
SCALE_ROW0 = 96
SCALAR_COLS = 88
RAW_BYTES = PACK * NQ * 4
ALIGN = 256

FLOPS = 2 * NQ * N * D


def tile_attend_nrm_taylor_topk_kernel(tc, qT, k_words, k_scales, offs, out):
    nc = tc.nc
    with ExitStack() as ctx:
        keep = ctx.enter_context(tc.tile_pool(name="keep", bufs=1))
        shared = ctx.enter_context(tc.tile_pool(name="shared", bufs=1))
        psum = ctx.enter_context(tc.psum_pool(name="psum", bufs=1))

        scale_pool = keep.tile([P, T // 4], I32, name="scale_pool", align_bytes=ALIGN)
        nc.sync.dma_start(scale_pool[SCALE_ROW0:P, :], k_scales.bitcast(I32).rearrange("o f t -> f o t"))
        offsets = keep.tile([P, N // 16], U16, name="offsets")
        nc.sync.dma_start(offsets[:], offs)
        word_pool = keep.tile([P, T], I32, name="word_pool", align_bytes=ALIGN)
        nc.sync.dma_start(word_pool[:], k_words[0].rearrange("p t b -> p (t b)").bitcast(I32))
        raws = []
        for o in range(PASSES):
            raw = shared.tile([P, PACK, NQ], F32, name=f"q_raw{o}", offset=o * RAW_BYTES, align_bytes=ALIGN)
            rows = qT[0, o * K_PASS : (o + 1) * K_PASS, :]
            nc.sync.dma_start(raw[:], rows.rearrange("(p j) w -> p j w", j=PACK))
            raws.append(raw)

        nc.vector.memset(scale_pool[0:SCALE_ROW0, :], 0)
        both_planes = keep.tile([P, PASSES, N // 4], I32, name="both_planes", align_bytes=ALIGN)
        nc.vector.memset(both_planes[:], 0)
        sums = keep.tile([P, GROUPS], F32, name="sums")
        one = keep.tile([P, 1], F32, name="one")
        nc.vector.memset(one[:], 1.0)
        nc.scalar.activation(sums[:, GROUPS - 1 : GROUPS], one[:], INV_SQRT, scale=1.0 / N**2)

        picked_scales = keep.tile([P, N], U8, name="picked_scales", align_bytes=ALIGN)
        nc.vector.tensor_copy(picked_scales[:], scale_pool[:].bitcast(U8).indirect(offsets[:]))
        for quad in range(4):
            first = SCALE_ROW0 + 8 * quad
            (nc.sync, nc.scalar)[quad % 2].dma_start(
                both_planes[32 * quad : 32 * quad + 4, :, :], picked_scales[:].bitcast(I32)[first : first + 8, :]
            )
        planes = [both_planes[:, o, :].bitcast(U8) for o in range(PASSES)]

        def round_queries(copy, o, cols):
            copy(
                groupeds[o][:, cols, :].rearrange("p (c i) t -> p c t i", i=2),
                raws[o][:, :, cols].rearrange("p t (c i) -> p c t i", i=2),
            )

        def quantize_queries(o):
            codes = keep.tile([P, NQ], U32, name=f"q_codes{o}", align_bytes=ALIGN)
            scales = keep.tile([P, NQ], U8, name=f"q_scales{o}", align_bytes=ALIGN)
            nc.vector.quantize_mx(
                out=codes[:].bitcast(FP8X4), scales=scales[:], in_=groupeds[o][:].rearrange("p w j -> p (w j)")
            )
            return codes, scales

        groupeds = [keep.tile([P, NQ, PACK], BF16, name=f"q_grouped{o}", align_bytes=ALIGN) for o in range(PASSES)]
        round_queries(nc.scalar.copy, 0, slice(0, NQ))
        round_queries(nc.scalar.copy, 1, slice(0, SCALAR_COLS))

        picked = {}
        for groups in (range(1), range(1, GROUPS)):
            words = keep.tile([P, len(groups) * GROUP], U32, name=f"picked_words{groups[0]}", align_bytes=ALIGN)
            cols = slice(groups[0] * GROUP // 16, (groups[-1] + 1) * GROUP // 16)
            nc.vector.tensor_copy(words[:], word_pool[:].bitcast(U32).indirect(offsets[:, cols]))
            halves = words[:].bitcast(U16).rearrange("p (n o) -> p o n", o=PASSES)
            for i, g in enumerate(groups):
                picked[g] = halves[:, :, i * GROUP :]

        keys = {}

        def part(passes, groups, tile):
            width = len(groups) * GROUP
            nc.vector.tensor_copy(
                tile[:].bitcast(U16).rearrange("p (o n) -> p o n", n=width),
                picked[groups[0]][:, passes[0] : passes[-1] + 1, :width],
            )
            for i, o in enumerate(passes):
                for j, g in enumerate(groups):
                    at = 2 * (i * width + j * GROUP)
                    keys[o, g] = tile[:, at : at + 2 * GROUP]

        def late_tile(name, units, offset):
            return shared.tile([P, 2 * GROUP * units], U8, name=name, offset=offset, align_bytes=ALIGN)

        part((0,), (0,), keep.tile([P, 2 * GROUP], U8, name="keys_a", align_bytes=ALIGN))
        round_queries(nc.vector.tensor_copy, 1, slice(SCALAR_COLS, NQ))
        queries = [quantize_queries(0)]
        part((0,), (1, 2), late_tile("keys_b", 2, 0))
        part((1,), (0,), late_tile("keys_c", 1, 4 * GROUP))
        queries.append(quantize_queries(1))
        part((1,), (1, 2), late_tile("keys_d", 2, RAW_BYTES))
        part((0, 1), (3,), late_tile("keys_e", 2, RAW_BYTES + 6 * GROUP))

        squares = keep.tile([P, N], F32, name="squares", align_bytes=ALIGN)
        banks = [psum.tile([P, GROUP], F32, name=f"scores{g}") for g in range(GROUPS)]
        for groups in (range(GROUPS - 1), range(GROUPS - 1, GROUPS)):
            for o in range(PASSES):
                for g in groups:
                    nc.tensor.matmul_mx(
                        out=banks[g][:],
                        lhsT=queries[o][0][:].bitcast(FP8X4),
                        lhsT_scale=queries[o][1][:],
                        rhs=keys[o, g].bitcast(FP4X4),
                        rhs_scale=planes[o][:, g * GROUP : (g + 1) * GROUP],
                        start=(o == 0),
                        stop=(o == PASSES - 1),
                    )
        last_sum = keep.tile([P, 1], F32, name="last_sum")
        for g in range(GROUPS):
            total = sums[:, g : g + 1] if g < GROUPS - 1 else last_sum[:]
            nc.scalar.activation(
                squares[:, g * GROUP : (g + 1) * GROUP], banks[g][:], SQUARE, bias=1.0, accum_out=total
            )

        numerators = keep.tile([P, N], F32, name="numerators", align_bytes=ALIGN)
        nc.vector.tensor_scalar_add(numerators[:, :HALF], squares[:, :HALF], 1.0)
        early_sum = keep.tile([P, 1], F32, name="early_sum")
        sums_again = keep.tile([P, GROUPS], F32, name="sums_again")
        nc.scalar.activation(sums_again[:], sums[:], COPY, accum_out=early_sum[:])
        for g in range(2, GROUPS):
            cols = slice(g * GROUP, (g + 1) * GROUP)
            nc.vector.tensor_scalar_add(numerators[:, cols], squares[:, cols], 1.0)
        root = keep.tile([P, 1], F32, name="root")
        nc.scalar.activation(root[:], last_sum[:], INV_SQRT, bias=early_sum[:])
        weights = keep.tile([P, N], F32, name="weights", align_bytes=ALIGN)
        for cols in (slice(0, N - GROUP), slice(N - GROUP, N)):
            nc.vector.tensor_scalar(weights[:, cols], numerators[:, cols], root[:], root[:], MULT, MULT)
        nc.sync.dma_start(out[0], weights[:])
